import numpy as np
import ml_dtypes


def mxq(x, axis, fmt="e4m3"):
    dtype, down = {"e4m3": (ml_dtypes.float8_e4m3fn, 7), "e5m2": (ml_dtypes.float8_e5m2, 14)}[fmt]
    v = np.moveaxis(np.asarray(x, np.float32).astype(ml_dtypes.bfloat16).astype(np.float64), axis, -1)
    blocks = v.reshape(v.shape[:-1] + (-1, 32))
    amax = np.abs(blocks).max(-1, keepdims=True)
    byte = np.maximum(np.where(amax > 0, np.frexp(amax)[1] - 1 + 127, 0) - down, 1)
    scale = np.exp2(byte - 127.0)
    codes = (blocks / scale).astype(np.float32).astype(dtype).astype(np.float64)
    return np.moveaxis((codes * scale).reshape(v.shape), -1, axis)


WIDE = False


def mx_kscale(k):
    if not WIDE:
        return np.ones(k)
    levels = np.array([10, -10, 5, -5, 0])
    if k % 512:
        return np.exp2(np.random.permutation(np.resize(levels, k // 32))).repeat(32)
    a = np.empty((k // 512, 16))
    for p in range(k // 512):
        a[p, :8] = np.random.permutation(np.resize(levels, 8))
        for g in range(8):
            far = levels[np.abs(levels - a[p, g]) >= 10]
            a[p, g + 8] = far[np.random.randint(len(far))]
    return np.exp2(a.ravel()).repeat(32)


def f64(x):
    return np.asarray(x).astype(np.float64)


def striped(idx):
    return np.tile(idx.reshape(-1, 16).T, (8, 1)).astype(np.uint16)


def unstriped(offs):
    return offs[:16].T.reshape(-1).astype(np.int64)


def striped8(idx):
    return np.concatenate([x.reshape(-1, 16).T for x in idx]).astype(np.uint16)


def runs(offs, k):
    lists = np.stack([offs[16 * r : 16 * r + 16].T.reshape(-1) for r in range(8)]).astype(np.int64)
    return lists[np.arange(k) % 512 // 64]


def pack_weight(w):
    k, n = w.shape
    w = f64(np.asarray(w, np.float32).astype(ml_dtypes.bfloat16)).reshape(k // 32, 32, n)
    amax = np.abs(w).max(1)
    byte = np.clip(np.where(amax > 0, np.frexp(amax)[1] - 1 + 127 - 7, 1), 1, 254)
    scaled = (w * np.exp2(127.0 - byte)[:, None, :]).reshape(k, n).astype(np.float32)
    words = np.ascontiguousarray(scaled.reshape(k // 512, 128, 4, n).transpose(0, 1, 3, 2)).astype(ml_dtypes.float8_e4m3fn).view(np.uint8)
    return words, np.ascontiguousarray(byte.astype(np.uint8).reshape(k // 512, 16, n))


def unpack_weight(words, scales):
    g, p, n, _ = words.shape
    vals = np.ascontiguousarray(words).view(ml_dtypes.float8_e4m3fn).astype(np.float64) * np.repeat(np.exp2(scales.astype(np.float64) - 127.0), 8, axis=1)[..., None]
    return vals.transpose(0, 1, 3, 2).reshape(g * 512, n)


K, T, S, N, H, W, C = 512, 2048, 512, 512, 512, 256, 512


def setup_inputs():
    n = np.random.standard_normal
    s = mx_kscale(K)[:, None]
    u = mx_kscale(S)
    packed_xT = pack_weight(n((K, T)) * s)
    perm = np.stack([np.random.permutation(S) for _ in range(8)])
    return {
        "x_words": packed_xT[0],
        "x_scales": packed_xT[1],
        "w1": (n((K, H)) / np.sqrt(K) / s).astype(np.float32),
        "gs": (np.random.uniform(0.5, 1.5, (K, 1)) / s).astype(np.float32),
        "res": (1.5 * n((N, S))).astype(np.float32),
        "gt": (np.random.uniform(0.5, 1.5, (C, 1)) * u[:, None]).astype(np.float32),
        "w2": (n((C, N)) / np.sqrt(C) / u[:, None]).astype(np.float32),
        "offs": striped(np.random.permutation(T)[:S]),
        "n1": striped8(perm[:, :W]),
        "n2": striped8(perm[:, W:]),
        "cand": striped(np.random.permutation(T)[:C]),
        "n3": striped8(np.stack([np.random.permutation(S) for _ in range(8)])),
        "n4": striped8(np.stack([np.random.permutation(S) for _ in range(8)])),
    }


def reference(x_words, x_scales, w1, gs, res, gt, w2, offs, n1, n2, cand, n3, n4):
    x_cand = unpack_weight(x_words, x_scales)[:, unstriped(cand)]
    xq = unpack_weight(x_words, x_scales)[:, unstriped(offs)]
    y = mxq(f64(w1), 0, "e4m3").T @ xq
    pa = y[np.arange(H)[:, None], runs(n1, H)]
    pb = y[np.arange(H)[:, None], runs(n2, H)]
    rb = np.maximum(0.5 * pa, pb)
    ra = pb - pa
    ds = np.zeros((H, S))
    ds[np.arange(H)[:, None], runs(n1, H)] = ra
    dt = ds.copy()
    dt[np.arange(H)[:, None], runs(n2, H)] = rb
    z = f64(gs) * dt
    s = 0.0625 * ((x_cand.T @ mxq(z, 0, "e4m3")))
    pa2 = s[np.arange(C)[:, None], runs(n3, C)]
    pb2 = s[np.arange(C)[:, None], runs(n4, C)]
    z2 = f64(gt) * (np.maximum(np.maximum(s, pa2), pb2) - (0.5 * (np.minimum(np.minimum(s, pa2), pb2))))
    return f64(res) + (mxq(f64(w2), 0, "e4m3").T @ mxq(z2, 0, "e4m3"))

@@ -1,0 +1,226 @@
+from contextlib import ExitStack
+
+import concourse.mybir as mybir
+
+F32 = mybir.dt.float32
+BF16 = mybir.dt.bfloat16
+I32 = mybir.dt.int32
+U32 = mybir.dt.uint32
+U16 = mybir.dt.uint16
+U8 = mybir.dt.uint8
+FP8X4 = mybir.dt.float8_e4m3fn_x4
+ALU = mybir.AluOpType
+COPY = mybir.ActivationFunctionType.Copy
+
+P = 128
+PACK = 4
+T = 2048
+S = 512
+W = 256
+LANES = 16
+FLOPS = 3 * 2 * 512 * 512 * 512
+CHUNKS = ((0, 256), (256, 384), (384, 512))
+
+
+def tile_picked_readliftrange_none_p_kernel(
+    tc, x_words, x_scales, w1, gs, res, gt, w2, offs, n1, n2, cand, n3, n4, out
+):
+    nc = tc.nc
+    with ExitStack() as ctx:
+        keep = ctx.enter_context(tc.tile_pool(name="keep", bufs=1))
+        ring = ctx.enter_context(tc.tile_pool(name="ring", bufs=3))
+        psum = ctx.enter_context(tc.psum_pool(name="psum", bufs=1))
+
+        def load_list(name, src):
+            tile = keep.tile([P, src.shape[1]], U16, name=name)
+            nc.sync.dma_start(tile[:], src)
+            return tile
+
+        x_bytes = keep.tile([P, T], U8, name="x_bytes", align_bytes=64)
+        nc.vector.memset(x_bytes[:].bitcast(I32), 0)
+        for q in range(4):
+            nc.scalar.dma_start(x_bytes[32 * q : 32 * q + 4, :].bitcast(I32), x_scales[0, 4 * q : 4 * q + 4, :].bitcast(I32))
+        offs_sb = load_list("offs_sb", offs)
+        w1_raw = []
+        for h in range(2):
+            raw = keep.tile([P, PACK, S // 2], F32, name=f"w1_raw{h}")
+            nc.sync.dma_start(raw[:], w1.rearrange("(p j) c -> p j c", j=PACK)[:, :, h * 256 : (h + 1) * 256])
+            w1_raw.append(raw)
+        x_codes = keep.tile([P, T], I32, name="x_codes", align_bytes=64)
+        nc.sync.dma_start(x_codes[:], x_words[0].rearrange("p n t -> p (n t)").bitcast(I32))
+        cand_sb = load_list("cand_sb", cand)
+        n1_sb = load_list("n1_sb", n1)
+        n2_sb = load_list("n2_sb", n2)
+        gs_sb = keep.tile([P, PACK], F32, name="gs_sb")
+        nc.sync.dma_start(gs_sb[:], gs.rearrange("(p t) o -> p (t o)", t=PACK))
+        w2_raw = keep.tile([P, PACK, S], F32, name="w2_raw")
+        nc.sync.dma_start(w2_raw[:], w2.rearrange("(p j) c -> p j c", j=PACK))
+        n3_sb = load_list("n3_sb", n3)
+        n4_sb = load_list("n4_sb", n4)
+        gt_sb = keep.tile([P, PACK], F32, name="gt_sb")
+        nc.sync.dma_start(gt_sb[:], gt.rearrange("(p t) o -> p (t o)", t=PACK))
+        res_sb = keep.tile([P, PACK, S], F32, name="res_sb")
+        nc.sync.dma_start(res_sb[:], res.rearrange("(b p) j -> p b j", p=P))
+
+        offs_bytes = keep.tile([P, S], U8, name="offs_bytes", align_bytes=64)
+        nc.vector.tensor_copy(offs_bytes[:], x_bytes[:].indirect(offs_sb[:]))
+        cand_bytes = keep.tile([P, S], U8, name="cand_bytes", align_bytes=64)
+        nc.vector.tensor_copy(cand_bytes[:], x_bytes[:].indirect(cand_sb[:]))
+        cand_bytes_dealt = keep.tile([P, S], U8, name="cand_bytes_dealt", align_bytes=64)
+        nc.vector.tensor_copy(
+            cand_bytes_dealt[:].rearrange("p (t m) -> p m t", t=PACK), cand_bytes[:].rearrange("p (m t) -> p m t", t=PACK)
+        )
+
+        w1_bf = keep.tile([P, PACK * S], BF16, name="w1_bf", align_bytes=64)
+        w1_view = w1_bf[:].rearrange("p (t m j) -> p m t j", t=PACK, j=PACK)
+        for h in range(2):
+            nc.scalar.copy(w1_view[:, 64 * h : 64 * (h + 1)], w1_raw[h][:].rearrange("p j (m t) -> p m t j", t=PACK))
+        w1_codes = keep.tile([P, S], U32, name="w1_codes", align_bytes=64)
+        w1_bytes = keep.tile([P, S], U8, name="w1_bytes", align_bytes=64)
+        nc.vector.quantize_mx(out=w1_codes[:].bitcast(FP8X4), scales=w1_bytes[:], in_=w1_bf[:])
+
+        offs_codes = keep.tile([P, S], U32, name="offs_codes", align_bytes=64)
+        nc.vector.tensor_copy(offs_codes[:], x_codes[:].bitcast(U32).indirect(offs_sb[:]))
+        cand_codes = keep.tile([P, S], U32, name="cand_codes", align_bytes=64)
+        nc.vector.tensor_copy(cand_codes[:].rearrange("p (t m) -> p m t", t=PACK), x_codes[:].bitcast(U32).indirect(cand_sb[:]))
+
+        y = []
+        for t in range(PACK):
+            bank = psum.tile([P, S], F32, name=f"y_bank{t}", tag=f"bank_a{t}")
+            cols = slice(P * t, P * (t + 1))
+            nc.tensor.matmul_mx(
+                out=bank[:], lhsT=w1_codes[:, cols].bitcast(FP8X4), lhsT_scale=w1_bytes[:, cols],
+                rhs=offs_codes[:].bitcast(FP8X4), rhs_scale=offs_bytes[:], start=True, stop=True,
+            )
+            y_t = keep.tile([P, S], F32, name=f"y{t}")
+            nc.scalar.copy(y_t[:], bank[:])
+            y.append(y_t)
+
+        w2_bf = keep.tile([P, S, PACK], BF16, name="w2_bf", align_bytes=64)
+        for b in range(PACK):
+            cols = slice(P * b, P * (b + 1))
+            nc.scalar.copy(w2_bf[:, cols, :], w2_raw[:, :, cols].rearrange("p j c -> p c j"))
+        gt16 = keep.tile([P, PACK], F32, name="gt16")
+        nc.scalar.activation(gt16[:], gt_sb[:], COPY, scale=0.0625)
+
+        z_bf = [keep.tile([P, W, PACK], BF16, name=f"z_bf{h}", align_bytes=64) for h in range(2)]
+        pending = None
+
+        def finish_pairs(t, dt, rb):
+            nc.vector.tensor_copy(dt[:].indirect(n2_sb[:]), rb[:])
+            for h in range(2):
+                nc.scalar.activation(z_bf[h][:, :, t], dt[:, W * h : W * (h + 1)], COPY, scale=gs_sb[:, t : t + 1])
+
+        for t in range(PACK):
+            neg_pa = ring.tile([P, W], F32, name="neg_pa")
+            nc.vector.tensor_scalar(neg_pa[:], y[t][:].indirect(n1_sb[:]), -1.0, 0.0, ALU.mult, ALU.add)
+            pb = ring.tile([P, W], F32, name="pb")
+            nc.vector.tensor_copy(pb[:], y[t][:].indirect(n2_sb[:]))
+            if pending is not None:
+                finish_pairs(*pending)
+            rb = ring.tile([P, W], F32, name="rb")
+            nc.vector.scalar_tensor_tensor(rb[:], neg_pa[:], -0.5, pb[:], ALU.mult, ALU.max)
+            dt = keep.tile([P, S], F32, name=f"dt{t}")
+            nc.vector.tensor_tensor(dt[:].indirect(n1_sb[:]), pb[:], neg_pa[:], ALU.add)
+            pending = (t, dt, rb)
+        finish_pairs(*pending)
+
+        z_codes = keep.tile([P, S], U32, name="z_codes", align_bytes=64)
+        z_bytes = keep.tile([P, S], U8, name="z_bytes", align_bytes=64)
+        s_banks = [psum.tile([P, S], F32, name=f"s_bank{t}", tag=f"bank_b{t}") for t in range(PACK)]
+        for h in range(2):
+            half = slice(W * h, W * (h + 1))
+            nc.vector.quantize_mx(
+                out=z_codes[:, half].bitcast(FP8X4), scales=z_bytes[:, half], in_=z_bf[h][:].rearrange("p c j -> p (c j)")
+            )
+            for t in range(PACK):
+                cols = slice(P * t, P * (t + 1))
+                nc.tensor.matmul_mx(
+                    out=s_banks[t][:, half], lhsT=cand_codes[:, cols].bitcast(FP8X4), lhsT_scale=cand_bytes_dealt[:, cols],
+                    rhs=z_codes[:, half].bitcast(FP8X4), rhs_scale=z_bytes[:, half], start=True, stop=True,
+                )
+        s = []
+        for t in range(PACK):
+            s_t = keep.tile([P, S], F32, name=f"s{t}")
+            nc.scalar.copy(s_t[:], s_banks[t][:])
+            s.append(s_t)
+
+        w2_codes = keep.tile([P, S], U32, name="w2_codes", align_bytes=64)
+        w2_bytes = keep.tile([P, S], U8, name="w2_bytes", align_bytes=64)
+        nc.vector.quantize_mx(out=w2_codes[:].bitcast(FP8X4), scales=w2_bytes[:], in_=w2_bf[:].rearrange("p c j -> p (c j)"))
+
+        z2_bf = [keep.tile([P, hi - lo, PACK], BF16, name=f"z2_bf{c}", align_bytes=64) for c, (lo, hi) in enumerate(CHUNKS)]
+        out_view = out.rearrange("(b p) j -> p b j", p=P)
+        units = [(t, 0, S) for t in range(PACK - 1)] + [(PACK - 1, lo, hi) for lo, hi in CHUNKS]
+        state = {}
+
+        def fetch(t, lo, hi):
+            pa2 = ring.tile([P, S], F32, name="pa2")
+            pb2 = ring.tile([P, S], F32, name="pb2")
+            for dst, lst in ((pa2, n3_sb), (pb2, n4_sb)):
+                for a in range(lo, hi, W):
+                    b = min(a + W, hi)
+                    nc.vector.tensor_copy(dst[:, a:b], s[t][:].indirect(lst[:, a // LANES : b // LANES]))
+            state[t, lo] = (pa2, pb2)
+
+        def extremes(t, lo, hi):
+            pa2, pb2 = state[t, lo]
+            big2 = ring.tile([P, S], F32, name="big2")
+            nc.vector.tensor_tensor(big2[:, lo:hi], pa2[:, lo:hi], pb2[:, lo:hi], ALU.max)
+            small2 = ring.tile([P, S], F32, name="small2")
+            nc.vector.tensor_tensor(small2[:, lo:hi], pa2[:, lo:hi], pb2[:, lo:hi], ALU.min)
+            big3 = ring.tile([P, S], F32, name="big3")
+            nc.vector.tensor_tensor(big3[:, lo:hi], big2[:, lo:hi], s[t][:, lo:hi], ALU.max)
+            small3 = ring.tile([P, S], F32, name="small3")
+            nc.vector.tensor_tensor(small3[:, lo:hi], small2[:, lo:hi], s[t][:, lo:hi], ALU.min)
+            state[t, lo] = (big3, small3)
+
+        def combine(t, lo, hi):
+            big3, small3 = state[t, lo]
+            spread = ring.tile([P, S], F32, name="spread")
+            nc.vector.scalar_tensor_tensor(spread[:, lo:hi], small3[:, lo:hi], -0.5, big3[:, lo:hi], ALU.mult, ALU.add)
+            for c, (a, b) in enumerate(CHUNKS):
+                if lo <= a and b <= hi:
+                    nc.scalar.activation(z2_bf[c][:, :, t], spread[:, a:b], COPY, scale=gt16[:, t : t + 1])
+
+        def product(c):
+            lo, hi = CHUNKS[c]
+            n = hi - lo
+            codes = keep.tile([P, n], U32, name=f"z2_codes{c}", align_bytes=64)
+            scales = keep.tile([P, n], U8, name=f"z2_bytes{c}", align_bytes=64)
+            nc.vector.quantize_mx(out=codes[:].bitcast(FP8X4), scales=scales[:], in_=z2_bf[c][:].rearrange("p c j -> p (c j)"))
+            per_bank = S // n
+            banks = []
+            for g in range(PACK // per_bank):
+                bank = psum.tile([P, per_bank, n], F32, name=f"out_bank{c}_{g}", tag=f"bank_a{lo // P + g}")
+                for i in range(per_bank):
+                    cols = slice(P * (g * per_bank + i), P * (g * per_bank + i + 1))
+                    nc.tensor.matmul_mx(
+                        out=bank[:, i, :], lhsT=w2_codes[:, cols].bitcast(FP8X4), lhsT_scale=w2_bytes[:, cols],
+                        rhs=codes[:].bitcast(FP8X4), rhs_scale=scales[:], start=True, stop=True,
+                    )
+                banks.append(bank)
+            state[c] = banks
+
+        def finish(c):
+            lo, hi = CHUNKS[c]
+            n = hi - lo
+            per_bank = S // n
+            for g, bank in enumerate(state[c]):
+                blocks = slice(g * per_bank, (g + 1) * per_bank)
+                result = keep.tile([P, per_bank, n], F32, name=f"result{c}_{g}")
+                nc.vector.tensor_tensor(result[:], bank[:], res_sb[:, blocks, lo:hi], ALU.add)
+                nc.sync.dma_start(out_view[:, blocks, lo:hi], result[:])
+
+        first_chunk = PACK - 1
+        for step in range(len(units) + 5):
+            if step < len(units):
+                fetch(*units[step])
+            if 0 <= step - 2 < len(units):
+                combine(*units[step - 2])
+            if 0 <= step - 1 < len(units):
+                extremes(*units[step - 1])
+            if first_chunk <= step - 3 < len(units):
+                product(step - 3 - first_chunk)
+            if first_chunk <= step - 4 < len(units):
+                finish(step - 4 - first_chunk)

@@ -1,6 +1,7 @@
 from contextlib import ExitStack
 
 import concourse.mybir as mybir
+from concourse.masks import make_identity
 
 F32 = mybir.dt.float32
 BF16 = mybir.dt.bfloat16
@@ -11,6 +12,7 @@ U8 = mybir.dt.uint8
 FP8X4 = mybir.dt.float8_e4m3fn_x4
 ALU = mybir.AluOpType
 COPY = mybir.ActivationFunctionType.Copy
+RELU = mybir.ActivationFunctionType.Relu
 
 P = 128
 PACK = 4
@@ -38,14 +40,15 @@ def tile_picked_readliftrange_none_p_kernel(
 
         x_bytes = keep.tile([P, T], U8, name="x_bytes", align_bytes=64)
         nc.vector.memset(x_bytes[:].bitcast(I32), 0)
+        w1_raw = [keep.tile([P, PACK, S // 2], F32, name=f"w1_raw{h}") for h in range(2)]
+        w1_rows = w1.rearrange("(p j) c -> p j c", j=PACK)
+        nc.sync.dma_start(w1_raw[0][:], w1_rows[:, :, :W])
         for q in range(4):
-            nc.scalar.dma_start(x_bytes[32 * q : 32 * q + 4, :].bitcast(I32), x_scales[0, 4 * q : 4 * q + 4, :].bitcast(I32))
+            nc.sync.dma_start(x_bytes[32 * q : 32 * q + 4, :].bitcast(I32), x_scales[0, 4 * q : 4 * q + 4, :].bitcast(I32))
+        ident = keep.tile([P, P], F32, name="ident")
+        make_identity(nc, ident[:])
         offs_sb = load_list("offs_sb", offs)
-        w1_raw = []
-        for h in range(2):
-            raw = keep.tile([P, PACK, S // 2], F32, name=f"w1_raw{h}")
-            nc.sync.dma_start(raw[:], w1.rearrange("(p j) c -> p j c", j=PACK)[:, :, h * 256 : (h + 1) * 256])
-            w1_raw.append(raw)
+        nc.sync.dma_start(w1_raw[1][:], w1_rows[:, :, W:])
         x_codes = keep.tile([P, T], I32, name="x_codes", align_bytes=64)
         nc.sync.dma_start(x_codes[:], x_words[0].rearrange("p n t -> p (n t)").bitcast(I32))
         cand_sb = load_list("cand_sb", cand)
@@ -66,10 +69,6 @@ def tile_picked_readliftrange_none_p_kernel(
         nc.vector.tensor_copy(offs_bytes[:], x_bytes[:].indirect(offs_sb[:]))
         cand_bytes = keep.tile([P, S], U8, name="cand_bytes", align_bytes=64)
         nc.vector.tensor_copy(cand_bytes[:], x_bytes[:].indirect(cand_sb[:]))
-        cand_bytes_dealt = keep.tile([P, S], U8, name="cand_bytes_dealt", align_bytes=64)
-        nc.vector.tensor_copy(
-            cand_bytes_dealt[:].rearrange("p (t m) -> p m t", t=PACK), cand_bytes[:].rearrange("p (m t) -> p m t", t=PACK)
-        )
 
         w1_bf = keep.tile([P, PACK * S], BF16, name="w1_bf", align_bytes=64)
         w1_view = w1_bf[:].rearrange("p (t m j) -> p m t j", t=PACK, j=PACK)
@@ -84,6 +83,11 @@ def tile_picked_readliftrange_none_p_kernel(
         cand_codes = keep.tile([P, S], U32, name="cand_codes", align_bytes=64)
         nc.vector.tensor_copy(cand_codes[:].rearrange("p (t m) -> p m t", t=PACK), x_codes[:].bitcast(U32).indirect(cand_sb[:]))
 
+        cand_bytes_dealt = keep.tile([P, S], U8, name="cand_bytes_dealt", align_bytes=64)
+        nc.vector.tensor_copy(
+            cand_bytes_dealt[:].rearrange("p (t m) -> p m t", t=PACK), cand_bytes[:].rearrange("p (m t) -> p m t", t=PACK)
+        )
+
         y = []
         for t in range(PACK):
             bank = psum.tile([P, S], F32, name=f"y_bank{t}", tag=f"bank_a{t}")
@@ -92,42 +96,69 @@ def tile_picked_readliftrange_none_p_kernel(
                 out=bank[:], lhsT=w1_codes[:, cols].bitcast(FP8X4), lhsT_scale=w1_bytes[:, cols],
                 rhs=offs_codes[:].bitcast(FP8X4), rhs_scale=offs_bytes[:], start=True, stop=True,
             )
-            y_t = keep.tile([P, S], F32, name=f"y{t}")
-            nc.scalar.copy(y_t[:], bank[:])
+            y_t = keep.tile([P, S], F32, name=f"y{t}", align_bytes=64)
+            nc.scalar.activation(y_t[:], bank[:], COPY, scale=0.5)
             y.append(y_t)
 
-        w2_bf = keep.tile([P, S, PACK], BF16, name="w2_bf", align_bytes=64)
-        for b in range(PACK):
-            cols = slice(P * b, P * (b + 1))
-            nc.scalar.copy(w2_bf[:, cols, :], w2_raw[:, :, cols].rearrange("p j c -> p c j"))
-        gt16 = keep.tile([P, PACK], F32, name="gt16")
-        nc.scalar.activation(gt16[:], gt_sb[:], COPY, scale=0.0625)
+        half_gain = keep.tile([P, PACK], F32, name="half_gain")
+        nc.gpsimd.tensor_scalar(half_gain[:], gt_sb[:], 0.03125, 0.0, ALU.mult, ALU.add)
+        three_if_pos = keep.tile([P, PACK], F32, name="three_if_pos")
+        nc.gpsimd.tensor_scalar(three_if_pos[:], gt_sb[:], 0.0, 3.0, ALU.is_ge, ALU.mult)
+        top_w = keep.tile([P, PACK], F32, name="top_w")
+        nc.gpsimd.tensor_scalar(top_w[:], three_if_pos[:], 1.0, -1.0, ALU.mult, ALU.add)
+        low_w = keep.tile([P, PACK], F32, name="low_w")
+        nc.gpsimd.tensor_scalar(low_w[:], three_if_pos[:], -1.0, 2.0, ALU.mult, ALU.add)
 
         z_bf = [keep.tile([P, W, PACK], BF16, name=f"z_bf{h}", align_bytes=64) for h in range(2)]
-        pending = None
+        dt = [keep.tile([P, S], F32, name=f"dt{t}", align_bytes=64) for t in range(PACK)]
+        neg_pb, lift, minus_2gap, pb = {}, {}, {}, {}
 
-        def finish_pairs(t, dt, rb):
-            nc.vector.tensor_copy(dt[:].indirect(n2_sb[:]), rb[:])
+        def fetch_pb(t):
+            neg_pb[t] = ring.tile([P, W], F32, name="neg_pb")
+            nc.vector.tensor_scalar(neg_pb[t][:], y[t][:].indirect(n2_sb[:]), -2.0, 0.0, ALU.mult, ALU.add)
+            pb[t] = ring.tile([P, W], F32, name="pb")
+            nc.scalar.activation(pb[t][:], neg_pb[t][:], COPY, scale=-1.0)
+
+        def fetch_gap(t):
+            gap = ring.tile([P, W], F32, name="gap")
+            nc.vector.tensor_tensor(gap[:], y[t][:].indirect(n1_sb[:]), neg_pb[t][:], ALU.add)
+            minus_2gap[t] = ring.tile([P, W], F32, name="minus_2gap")
+            nc.scalar.activation(minus_2gap[t][:], gap[:], COPY, scale=-2.0)
+            lift[t] = ring.tile([P, W], F32, name="lift")
+            nc.scalar.activation(lift[t][:], gap[:], RELU)
+
+        def put_ra(t):
+            nc.vector.tensor_tensor(dt[t][:].indirect(n1_sb[:]), neg_pb[t][:], minus_2gap[t][:], ALU.add)
+
+        def put_rb(t):
+            nc.vector.tensor_tensor(dt[t][:].indirect(n2_sb[:]), pb[t][:], lift[t][:], ALU.add)
             for h in range(2):
-                nc.scalar.activation(z_bf[h][:, :, t], dt[:, W * h : W * (h + 1)], COPY, scale=gs_sb[:, t : t + 1])
+                if h == 1 or t < 2:
+                    nc.scalar.activation(z_bf[h][:, :, t], dt[t][:, W * h : W * (h + 1)], COPY, scale=gs_sb[:, t : t + 1])
 
-        for t in range(PACK):
-            neg_pa = ring.tile([P, W], F32, name="neg_pa")
-            nc.vector.tensor_scalar(neg_pa[:], y[t][:].indirect(n1_sb[:]), -1.0, 0.0, ALU.mult, ALU.add)
-            pb = ring.tile([P, W], F32, name="pb")
-            nc.vector.tensor_copy(pb[:], y[t][:].indirect(n2_sb[:]))
-            if pending is not None:
-                finish_pairs(*pending)
-            rb = ring.tile([P, W], F32, name="rb")
-            nc.vector.scalar_tensor_tensor(rb[:], neg_pa[:], -0.5, pb[:], ALU.mult, ALU.max)
-            dt = keep.tile([P, S], F32, name=f"dt{t}")
-            nc.vector.tensor_tensor(dt[:].indirect(n1_sb[:]), pb[:], neg_pa[:], ALU.add)
-            pending = (t, dt, rb)
-        finish_pairs(*pending)
+        for t in range(2):
+            fetch_pb(t)
+        for t in range(2):
+            fetch_gap(t)
+        w2_bf = []
+        for t in range(2):
+            put_ra(t)
+            fetch_pb(t + 2)
+            put_rb(t)
+            fetch_gap(t + 2)
+            piece = keep.tile([P, W, PACK], BF16, name=f"w2_bf{t}", tag=f"y{t + 2}", align_bytes=64)
+            nc.scalar.copy(piece[:], w2_raw[:, :, W * t : W * (t + 1)].rearrange("p j c -> p c j"))
+            w2_bf.append(piece)
+        for put in (put_ra, put_rb):
+            for t in range(2, PACK):
+                put(t)
+        for t in range(2, PACK):
+            nc.vector.tensor_scalar(z_bf[0][:, :, t], dt[t][:, :W], gs_sb[:, t : t + 1], None, ALU.mult)
 
         z_codes = keep.tile([P, S], U32, name="z_codes", align_bytes=64)
         z_bytes = keep.tile([P, S], U8, name="z_bytes", align_bytes=64)
         s_banks = [psum.tile([P, S], F32, name=f"s_bank{t}", tag=f"bank_b{t}") for t in range(PACK)]
+        s_first = psum.tile([P, W], F32, name="s_first", tag="bank_a0")
         for h in range(2):
             half = slice(W * h, W * (h + 1))
             nc.vector.quantize_mx(
@@ -136,52 +167,85 @@ def tile_picked_readliftrange_none_p_kernel(
             for t in range(PACK):
                 cols = slice(P * t, P * (t + 1))
                 nc.tensor.matmul_mx(
-                    out=s_banks[t][:, half], lhsT=cand_codes[:, cols].bitcast(FP8X4), lhsT_scale=cand_bytes_dealt[:, cols],
+                    out=s_first[:] if t == 0 and h == 0 else s_banks[t][:, half], lhsT=cand_codes[:, cols].bitcast(FP8X4), lhsT_scale=cand_bytes_dealt[:, cols],
                     rhs=z_codes[:, half].bitcast(FP8X4), rhs_scale=z_bytes[:, half], start=True, stop=True,
                 )
-        s = []
-        for t in range(PACK):
-            s_t = keep.tile([P, S], F32, name=f"s{t}")
-            nc.scalar.copy(s_t[:], s_banks[t][:])
-            s.append(s_t)
-
-        w2_codes = keep.tile([P, S], U32, name="w2_codes", align_bytes=64)
+        w2_codes = keep.tile([P, S], U32, name="w2_codes", tag="dt3", align_bytes=64)
         w2_bytes = keep.tile([P, S], U8, name="w2_bytes", align_bytes=64)
-        nc.vector.quantize_mx(out=w2_codes[:].bitcast(FP8X4), scales=w2_bytes[:], in_=w2_bf[:].rearrange("p c j -> p (c j)"))
+        for h in range(2):
+            half = slice(W * h, W * (h + 1))
+            nc.vector.quantize_mx(
+                out=w2_codes[:, half].bitcast(FP8X4), scales=w2_bytes[:, half], in_=w2_bf[h][:].rearrange("p c j -> p (c j)")
+            )
 
-        z2_bf = [keep.tile([P, hi - lo, PACK], BF16, name=f"z2_bf{c}", align_bytes=64) for c, (lo, hi) in enumerate(CHUNKS)]
+        s = [keep.tile([P, S], F32, name=f"s{t}") for t in range(PACK)]
+        s_plain = [keep.tile([P, S], F32, name=f"s_plain{t}") for t in range(PACK)]
+        gain0 = half_gain[:, 0:1]
+        nc.scalar.activation(s[0][:, :W], s_first[:], COPY, scale=gain0)
+        nc.vector.tensor_copy(s_plain[0][:, :W], s[0][:, :W])
+        nc.scalar.activation(s[0][:, W:], s_banks[0][:, W:], COPY, scale=gain0)
+        nc.scalar.activation(s_plain[0][:, W:], s_banks[0][:, W:], COPY, scale=gain0)
+        for t in range(1, PACK):
+            for dst in (s[t], s_plain[t]):
+                nc.scalar.activation(dst[:], s_banks[t][:], COPY, scale=half_gain[:, t : t + 1])
+
         out_view = out.rearrange("(b p) j -> p b j", p=P)
-        units = [(t, 0, S) for t in range(PACK - 1)] + [(PACK - 1, lo, hi) for lo, hi in CHUNKS]
+        units = [(0, 0, S), (1, 0, S), (2, 0, W), (3, 0, W), (2, W, S)] + [(3, lo, hi) for lo, hi in CHUNKS[1:]]
         state = {}
+        sums = {}
+        for u, tags in enumerate((("bank_a0", "bank_a1", None), ("bank_a2", "bank_a3", "bank_b0"))):
+            for c, (lo, hi) in enumerate(CHUNKS):
+                if tags[c] is not None:
+                    bank = psum.tile([P, 2, 2, P], F32, name=f"sum_bank{u}_{c}", tag=tags[c])
+                    sums[u, c] = bank[:, : (hi - lo) // P]
+                else:
+                    sums[u, c] = bank[:, 1:2]
+        word_banks = [psum.tile([P, 2, hi - lo], F32, name=f"word_bank{c}", tag=f"bank_b{c + 1}") for c, (lo, hi) in enumerate(CHUNKS)]
+        z2_bf = [keep.tile([P, hi - lo, PACK], BF16, name=f"z2_bf{c}", align_bytes=64) for c, (lo, hi) in enumerate(CHUNKS)]
 
         def fetch(t, lo, hi):
-            pa2 = ring.tile([P, S], F32, name="pa2")
-            pb2 = ring.tile([P, S], F32, name="pb2")
-            for dst, lst in ((pa2, n3_sb), (pb2, n4_sb)):
+            da = ring.tile([P, S], F32, name="da")
+            db = ring.tile([P, S], F32, name="db")
+            for dst, lst in ((da, n3_sb), (db, n4_sb)):
                 for a in range(lo, hi, W):
                     b = min(a + W, hi)
-                    nc.vector.tensor_copy(dst[:, a:b], s[t][:].indirect(lst[:, a // LANES : b // LANES]))
-            state[t, lo] = (pa2, pb2)
+                    nc.vector.tensor_tensor(dst[:, a:b], s[t][:].indirect(lst[:, a // LANES : b // LANES]), s_plain[t][:, a:b], ALU.subtract)
+            state[t, lo] = (da, db)
 
         def extremes(t, lo, hi):
-            pa2, pb2 = state[t, lo]
-            big2 = ring.tile([P, S], F32, name="big2")
-            nc.vector.tensor_tensor(big2[:, lo:hi], pa2[:, lo:hi], pb2[:, lo:hi], ALU.max)
-            small2 = ring.tile([P, S], F32, name="small2")
-            nc.vector.tensor_tensor(small2[:, lo:hi], pa2[:, lo:hi], pb2[:, lo:hi], ALU.min)
-            big3 = ring.tile([P, S], F32, name="big3")
-            nc.vector.tensor_tensor(big3[:, lo:hi], big2[:, lo:hi], s[t][:, lo:hi], ALU.max)
-            small3 = ring.tile([P, S], F32, name="small3")
-            nc.vector.tensor_tensor(small3[:, lo:hi], small2[:, lo:hi], s[t][:, lo:hi], ALU.min)
-            state[t, lo] = (big3, small3)
-
-        def combine(t, lo, hi):
-            big3, small3 = state[t, lo]
-            spread = ring.tile([P, S], F32, name="spread")
-            nc.vector.scalar_tensor_tensor(spread[:, lo:hi], small3[:, lo:hi], -0.5, big3[:, lo:hi], ALU.mult, ALU.add)
+            da, db = state[t, lo]
+            top = ring.tile([P, S], F32, name="top")
+            nc.vector.scalar_tensor_tensor(top[:, lo:hi], da[:, lo:hi], 0.0, db[:, lo:hi], ALU.max, ALU.max)
+            low = ring.tile([P, S], F32, name="low")
+            nc.vector.scalar_tensor_tensor(low[:, lo:hi], da[:, lo:hi], 0.0, db[:, lo:hi], ALU.min, ALU.min)
+            top_term = ring.tile([P, S], F32, name="top_term")
+            nc.scalar.activation(top_term[:, lo:hi], top[:, lo:hi], COPY, scale=top_w[:, t : t + 1])
+            low_term = ring.tile([P, S], F32, name="low_term")
+            nc.scalar.activation(low_term[:, lo:hi], low[:, lo:hi], COPY, scale=low_w[:, t : t + 1])
+            u, e = divmod(t, 2)
+            terms = (s_plain[t], top_term, low_term)
             for c, (a, b) in enumerate(CHUNKS):
                 if lo <= a and b <= hi:
-                    nc.scalar.activation(z2_bf[c][:, :, t], spread[:, a:b], COPY, scale=gt16[:, t : t + 1])
+                    for blk in range((b - a) // P):
+                        cols = slice(a + P * blk, a + P * (blk + 1))
+                        for k, term in enumerate(terms):
+                            nc.tensor.matmul(
+                                sums[u, c][:, blk, e, :], lhsT=term[:, cols], rhs=ident[:],
+                                is_transpose=True, start=(k == 0), stop=(k == len(terms) - 1),
+                            )
+            for c, (a, b) in enumerate(CHUNKS):
+                if e == 1 and lo <= a and b <= hi:
+                    nblk = (b - a) // P
+                    turned = keep.tile([P, nblk, P, 2], BF16, name=f"turned{u}_{c}")
+                    nc.scalar.copy(turned[:], sums[u, c].rearrange("j b e p -> j b p e"))
+                    words = turned[:].rearrange("j b p e -> j (b p e)").bitcast(F32)
+                    for blk in range(nblk):
+                        nc.tensor.transpose(word_banks[c][:, u, P * blk : P * (blk + 1)], words[:, P * blk : P * (blk + 1)], ident[:])
+                    if u == 1:
+                        nc.scalar.copy(
+                            z2_bf[c][:].rearrange("p j t -> p (j t)").bitcast(F32).rearrange("p (j u) -> p j u", u=2),
+                            word_banks[c][:].rearrange("p u j -> p j u"),
+                        )
 
         def product(c):
             lo, hi = CHUNKS[c]
@@ -206,21 +270,21 @@ def tile_picked_readliftrange_none_p_kernel(
             lo, hi = CHUNKS[c]
             n = hi - lo
             per_bank = S // n
-            for g, bank in enumerate(state[c]):
-                blocks = slice(g * per_bank, (g + 1) * per_bank)
-                result = keep.tile([P, per_bank, n], F32, name=f"result{c}_{g}")
-                nc.vector.tensor_tensor(result[:], bank[:], res_sb[:, blocks, lo:hi], ALU.add)
-                nc.sync.dma_start(out_view[:, blocks, lo:hi], result[:])
+            rows = [bank[:, i : i + 2] for bank in state[c] for i in range(0, per_bank, 2)]
+            for g, part in enumerate(rows):
+                blocks = slice(2 * g, 2 * (g + 1))
+                result = keep.tile([P, 2, n], F32, name=f"result{c}_{g}")
+                nc.vector.tensor_tensor(result[:], part, res_sb[:, blocks, lo:hi], ALU.add)
+                queue = nc.scalar if c == len(CHUNKS) - 1 and g == 0 else nc.sync
+                queue.dma_start(out_view[:, blocks, lo:hi], result[:])
 
-        first_chunk = PACK - 1
-        for step in range(len(units) + 5):
+        closes = {units.index((3, lo, hi)): c for c, (lo, hi) in enumerate(CHUNKS)}
+        for step in range(len(units) + 3):
             if step < len(units):
                 fetch(*units[step])
-            if 0 <= step - 2 < len(units):
-                combine(*units[step - 2])
             if 0 <= step - 1 < len(units):
                 extremes(*units[step - 1])
-            if first_chunk <= step - 3 < len(units):
-                product(step - 3 - first_chunk)
-            if first_chunk <= step - 4 < len(units):
-                finish(step - 4 - first_chunk)
+            if step - 2 in closes:
+                product(closes[step - 2])
+            if step - 3 in closes:
+                finish(closes[step - 3])

from contextlib import ExitStack

import concourse.mybir as mybir
from concourse.masks import make_identity

F32 = mybir.dt.float32
BF16 = mybir.dt.bfloat16
I32 = mybir.dt.int32
U32 = mybir.dt.uint32
U16 = mybir.dt.uint16
U8 = mybir.dt.uint8
FP8X4 = mybir.dt.float8_e4m3fn_x4
ALU = mybir.AluOpType
COPY = mybir.ActivationFunctionType.Copy
RELU = mybir.ActivationFunctionType.Relu

P = 128
PACK = 4
T = 2048
S = 512
W = 256
LANES = 16
FLOPS = 3 * 2 * 512 * 512 * 512
CHUNKS = ((0, 256), (256, 384), (384, 512))


def tile_picked_readliftrange_none_p_kernel(
    tc, x_words, x_scales, w1, gs, res, gt, w2, offs, n1, n2, cand, n3, n4, out
):
    nc = tc.nc
    with ExitStack() as ctx:
        keep = ctx.enter_context(tc.tile_pool(name="keep", bufs=1))
        ring = ctx.enter_context(tc.tile_pool(name="ring", bufs=3))
        psum = ctx.enter_context(tc.psum_pool(name="psum", bufs=1))

        def load_list(name, src):
            tile = keep.tile([P, src.shape[1]], U16, name=name)
            nc.sync.dma_start(tile[:], src)
            return tile

        x_bytes = keep.tile([P, T], U8, name="x_bytes", align_bytes=64)
        nc.vector.memset(x_bytes[:].bitcast(I32), 0)
        w1_raw = [keep.tile([P, PACK, S // 2], F32, name=f"w1_raw{h}") for h in range(2)]
        w1_rows = w1.rearrange("(p j) c -> p j c", j=PACK)
        nc.sync.dma_start(w1_raw[0][:], w1_rows[:, :, :W])
        for q in range(4):
            nc.sync.dma_start(x_bytes[32 * q : 32 * q + 4, :].bitcast(I32), x_scales[0, 4 * q : 4 * q + 4, :].bitcast(I32))
        ident = keep.tile([P, P], F32, name="ident")
        make_identity(nc, ident[:])
        offs_sb = load_list("offs_sb", offs)
        nc.sync.dma_start(w1_raw[1][:], w1_rows[:, :, W:])
        x_codes = keep.tile([P, T], I32, name="x_codes", align_bytes=64)
        nc.sync.dma_start(x_codes[:], x_words[0].rearrange("p n t -> p (n t)").bitcast(I32))
        cand_sb = load_list("cand_sb", cand)
        n1_sb = load_list("n1_sb", n1)
        n2_sb = load_list("n2_sb", n2)
        gs_sb = keep.tile([P, PACK], F32, name="gs_sb")
        nc.sync.dma_start(gs_sb[:], gs.rearrange("(p t) o -> p (t o)", t=PACK))
        w2_raw = keep.tile([P, PACK, S], F32, name="w2_raw")
        nc.sync.dma_start(w2_raw[:], w2.rearrange("(p j) c -> p j c", j=PACK))
        n3_sb = load_list("n3_sb", n3)
        n4_sb = load_list("n4_sb", n4)
        gt_sb = keep.tile([P, PACK], F32, name="gt_sb")
        nc.sync.dma_start(gt_sb[:], gt.rearrange("(p t) o -> p (t o)", t=PACK))
        res_sb = keep.tile([P, PACK, S], F32, name="res_sb")
        nc.sync.dma_start(res_sb[:], res.rearrange("(b p) j -> p b j", p=P))

        offs_bytes = keep.tile([P, S], U8, name="offs_bytes", align_bytes=64)
        nc.vector.tensor_copy(offs_bytes[:], x_bytes[:].indirect(offs_sb[:]))
        cand_bytes = keep.tile([P, S], U8, name="cand_bytes", align_bytes=64)
        nc.vector.tensor_copy(cand_bytes[:], x_bytes[:].indirect(cand_sb[:]))

        w1_bf = keep.tile([P, PACK * S], BF16, name="w1_bf", align_bytes=64)
        w1_view = w1_bf[:].rearrange("p (t m j) -> p m t j", t=PACK, j=PACK)
        for h in range(2):
            nc.scalar.copy(w1_view[:, 64 * h : 64 * (h + 1)], w1_raw[h][:].rearrange("p j (m t) -> p m t j", t=PACK))
        w1_codes = keep.tile([P, S], U32, name="w1_codes", align_bytes=64)
        w1_bytes = keep.tile([P, S], U8, name="w1_bytes", align_bytes=64)
        nc.vector.quantize_mx(out=w1_codes[:].bitcast(FP8X4), scales=w1_bytes[:], in_=w1_bf[:])

        offs_codes = keep.tile([P, S], U32, name="offs_codes", align_bytes=64)
        nc.vector.tensor_copy(offs_codes[:], x_codes[:].bitcast(U32).indirect(offs_sb[:]))
        cand_codes = keep.tile([P, S], U32, name="cand_codes", align_bytes=64)
        nc.vector.tensor_copy(cand_codes[:].rearrange("p (t m) -> p m t", t=PACK), x_codes[:].bitcast(U32).indirect(cand_sb[:]))

        cand_bytes_dealt = keep.tile([P, S], U8, name="cand_bytes_dealt", align_bytes=64)
        nc.vector.tensor_copy(
            cand_bytes_dealt[:].rearrange("p (t m) -> p m t", t=PACK), cand_bytes[:].rearrange("p (m t) -> p m t", t=PACK)
        )

        y = []
        for t in range(PACK):
            bank = psum.tile([P, S], F32, name=f"y_bank{t}", tag=f"bank_a{t}")
            cols = slice(P * t, P * (t + 1))
            nc.tensor.matmul_mx(
                out=bank[:], lhsT=w1_codes[:, cols].bitcast(FP8X4), lhsT_scale=w1_bytes[:, cols],
                rhs=offs_codes[:].bitcast(FP8X4), rhs_scale=offs_bytes[:], start=True, stop=True,
            )
            y_t = keep.tile([P, S], F32, name=f"y{t}", align_bytes=64)
            nc.scalar.activation(y_t[:], bank[:], COPY, scale=0.5)
            y.append(y_t)

        half_gain = keep.tile([P, PACK], F32, name="half_gain")
        nc.gpsimd.tensor_scalar(half_gain[:], gt_sb[:], 0.03125, 0.0, ALU.mult, ALU.add)
        three_if_pos = keep.tile([P, PACK], F32, name="three_if_pos")
        nc.gpsimd.tensor_scalar(three_if_pos[:], gt_sb[:], 0.0, 3.0, ALU.is_ge, ALU.mult)
        top_w = keep.tile([P, PACK], F32, name="top_w")
        nc.gpsimd.tensor_scalar(top_w[:], three_if_pos[:], 1.0, -1.0, ALU.mult, ALU.add)
        low_w = keep.tile([P, PACK], F32, name="low_w")
        nc.gpsimd.tensor_scalar(low_w[:], three_if_pos[:], -1.0, 2.0, ALU.mult, ALU.add)

        z_bf = [keep.tile([P, W, PACK], BF16, name=f"z_bf{h}", align_bytes=64) for h in range(2)]
        dt = [keep.tile([P, S], F32, name=f"dt{t}", align_bytes=64) for t in range(PACK)]
        neg_pb, lift, minus_2gap, pb = {}, {}, {}, {}

        def fetch_pb(t):
            neg_pb[t] = ring.tile([P, W], F32, name="neg_pb")
            nc.vector.tensor_scalar(neg_pb[t][:], y[t][:].indirect(n2_sb[:]), -2.0, 0.0, ALU.mult, ALU.add)
            pb[t] = ring.tile([P, W], F32, name="pb")
            nc.scalar.activation(pb[t][:], neg_pb[t][:], COPY, scale=-1.0)

        def fetch_gap(t):
            gap = ring.tile([P, W], F32, name="gap")
            nc.vector.tensor_tensor(gap[:], y[t][:].indirect(n1_sb[:]), neg_pb[t][:], ALU.add)
            minus_2gap[t] = ring.tile([P, W], F32, name="minus_2gap")
            nc.scalar.activation(minus_2gap[t][:], gap[:], COPY, scale=-2.0)
            lift[t] = ring.tile([P, W], F32, name="lift")
            nc.scalar.activation(lift[t][:], gap[:], RELU)

        def put_ra(t):
            nc.vector.tensor_tensor(dt[t][:].indirect(n1_sb[:]), neg_pb[t][:], minus_2gap[t][:], ALU.add)

        def put_rb(t):
            nc.vector.tensor_tensor(dt[t][:].indirect(n2_sb[:]), pb[t][:], lift[t][:], ALU.add)
            for h in range(2):
                if h == 1 or t < 2:
                    nc.scalar.activation(z_bf[h][:, :, t], dt[t][:, W * h : W * (h + 1)], COPY, scale=gs_sb[:, t : t + 1])

        for t in range(2):
            fetch_pb(t)
        for t in range(2):
            fetch_gap(t)
        w2_bf = []
        for t in range(2):
            put_ra(t)
            fetch_pb(t + 2)
            put_rb(t)
            fetch_gap(t + 2)
            piece = keep.tile([P, W, PACK], BF16, name=f"w2_bf{t}", tag=f"y{t + 2}", align_bytes=64)
            nc.scalar.copy(piece[:], w2_raw[:, :, W * t : W * (t + 1)].rearrange("p j c -> p c j"))
            w2_bf.append(piece)
        for put in (put_ra, put_rb):
            for t in range(2, PACK):
                put(t)
        for t in range(2, PACK):
            nc.vector.tensor_scalar(z_bf[0][:, :, t], dt[t][:, :W], gs_sb[:, t : t + 1], None, ALU.mult)

        z_codes = keep.tile([P, S], U32, name="z_codes", align_bytes=64)
        z_bytes = keep.tile([P, S], U8, name="z_bytes", align_bytes=64)
        s_banks = [psum.tile([P, S], F32, name=f"s_bank{t}", tag=f"bank_b{t}") for t in range(PACK)]
        s_first = psum.tile([P, W], F32, name="s_first", tag="bank_a0")
        for h in range(2):
            half = slice(W * h, W * (h + 1))
            nc.vector.quantize_mx(
                out=z_codes[:, half].bitcast(FP8X4), scales=z_bytes[:, half], in_=z_bf[h][:].rearrange("p c j -> p (c j)")
            )
            for t in range(PACK):
                cols = slice(P * t, P * (t + 1))
                nc.tensor.matmul_mx(
                    out=s_first[:] if t == 0 and h == 0 else s_banks[t][:, half], lhsT=cand_codes[:, cols].bitcast(FP8X4), lhsT_scale=cand_bytes_dealt[:, cols],
                    rhs=z_codes[:, half].bitcast(FP8X4), rhs_scale=z_bytes[:, half], start=True, stop=True,
                )
        w2_codes = keep.tile([P, S], U32, name="w2_codes", tag="dt3", align_bytes=64)
        w2_bytes = keep.tile([P, S], U8, name="w2_bytes", align_bytes=64)
        for h in range(2):
            half = slice(W * h, W * (h + 1))
            nc.vector.quantize_mx(
                out=w2_codes[:, half].bitcast(FP8X4), scales=w2_bytes[:, half], in_=w2_bf[h][:].rearrange("p c j -> p (c j)")
            )

        s = [keep.tile([P, S], F32, name=f"s{t}") for t in range(PACK)]
        s_plain = [keep.tile([P, S], F32, name=f"s_plain{t}") for t in range(PACK)]
        gain0 = half_gain[:, 0:1]
        nc.scalar.activation(s[0][:, :W], s_first[:], COPY, scale=gain0)
        nc.vector.tensor_copy(s_plain[0][:, :W], s[0][:, :W])
        nc.scalar.activation(s[0][:, W:], s_banks[0][:, W:], COPY, scale=gain0)
        nc.scalar.activation(s_plain[0][:, W:], s_banks[0][:, W:], COPY, scale=gain0)
        for t in range(1, PACK):
            for dst in (s[t], s_plain[t]):
                nc.scalar.activation(dst[:], s_banks[t][:], COPY, scale=half_gain[:, t : t + 1])

        out_view = out.rearrange("(b p) j -> p b j", p=P)
        units = [(0, 0, S), (1, 0, S), (2, 0, W), (3, 0, W), (2, W, S)] + [(3, lo, hi) for lo, hi in CHUNKS[1:]]
        state = {}
        sums = {}
        for u, tags in enumerate((("bank_a0", "bank_a1", None), ("bank_a2", "bank_a3", "bank_b0"))):
            for c, (lo, hi) in enumerate(CHUNKS):
                if tags[c] is not None:
                    bank = psum.tile([P, 2, 2, P], F32, name=f"sum_bank{u}_{c}", tag=tags[c])
                    sums[u, c] = bank[:, : (hi - lo) // P]
                else:
                    sums[u, c] = bank[:, 1:2]
        word_banks = [psum.tile([P, 2, hi - lo], F32, name=f"word_bank{c}", tag=f"bank_b{c + 1}") for c, (lo, hi) in enumerate(CHUNKS)]
        z2_bf = [keep.tile([P, hi - lo, PACK], BF16, name=f"z2_bf{c}", align_bytes=64) for c, (lo, hi) in enumerate(CHUNKS)]

        def fetch(t, lo, hi):
            da = ring.tile([P, S], F32, name="da")
            db = ring.tile([P, S], F32, name="db")
            for dst, lst in ((da, n3_sb), (db, n4_sb)):
                for a in range(lo, hi, W):
                    b = min(a + W, hi)
                    nc.vector.tensor_tensor(dst[:, a:b], s[t][:].indirect(lst[:, a // LANES : b // LANES]), s_plain[t][:, a:b], ALU.subtract)
            state[t, lo] = (da, db)

        def extremes(t, lo, hi):
            da, db = state[t, lo]
            top = ring.tile([P, S], F32, name="top")
            nc.vector.scalar_tensor_tensor(top[:, lo:hi], da[:, lo:hi], 0.0, db[:, lo:hi], ALU.max, ALU.max)
            low = ring.tile([P, S], F32, name="low")
            nc.vector.scalar_tensor_tensor(low[:, lo:hi], da[:, lo:hi], 0.0, db[:, lo:hi], ALU.min, ALU.min)
            top_term = ring.tile([P, S], F32, name="top_term")
            nc.scalar.activation(top_term[:, lo:hi], top[:, lo:hi], COPY, scale=top_w[:, t : t + 1])
            low_term = ring.tile([P, S], F32, name="low_term")
            nc.scalar.activation(low_term[:, lo:hi], low[:, lo:hi], COPY, scale=low_w[:, t : t + 1])
            u, e = divmod(t, 2)
            terms = (s_plain[t], top_term, low_term)
            for c, (a, b) in enumerate(CHUNKS):
                if lo <= a and b <= hi:
                    for blk in range((b - a) // P):
                        cols = slice(a + P * blk, a + P * (blk + 1))
                        for k, term in enumerate(terms):
                            nc.tensor.matmul(
                                sums[u, c][:, blk, e, :], lhsT=term[:, cols], rhs=ident[:],
                                is_transpose=True, start=(k == 0), stop=(k == len(terms) - 1),
                            )
            for c, (a, b) in enumerate(CHUNKS):
                if e == 1 and lo <= a and b <= hi:
                    nblk = (b - a) // P
                    turned = keep.tile([P, nblk, P, 2], BF16, name=f"turned{u}_{c}")
                    nc.scalar.copy(turned[:], sums[u, c].rearrange("j b e p -> j b p e"))
                    words = turned[:].rearrange("j b p e -> j (b p e)").bitcast(F32)
                    for blk in range(nblk):
                        nc.tensor.transpose(word_banks[c][:, u, P * blk : P * (blk + 1)], words[:, P * blk : P * (blk + 1)], ident[:])
                    if u == 1:
                        nc.scalar.copy(
                            z2_bf[c][:].rearrange("p j t -> p (j t)").bitcast(F32).rearrange("p (j u) -> p j u", u=2),
                            word_banks[c][:].rearrange("p u j -> p j u"),
                        )

        def product(c):
            lo, hi = CHUNKS[c]
            n = hi - lo
            codes = keep.tile([P, n], U32, name=f"z2_codes{c}", align_bytes=64)
            scales = keep.tile([P, n], U8, name=f"z2_bytes{c}", align_bytes=64)
            nc.vector.quantize_mx(out=codes[:].bitcast(FP8X4), scales=scales[:], in_=z2_bf[c][:].rearrange("p c j -> p (c j)"))
            per_bank = S // n
            banks = []
            for g in range(PACK // per_bank):
                bank = psum.tile([P, per_bank, n], F32, name=f"out_bank{c}_{g}", tag=f"bank_a{lo // P + g}")
                for i in range(per_bank):
                    cols = slice(P * (g * per_bank + i), P * (g * per_bank + i + 1))
                    nc.tensor.matmul_mx(
                        out=bank[:, i, :], lhsT=w2_codes[:, cols].bitcast(FP8X4), lhsT_scale=w2_bytes[:, cols],
                        rhs=codes[:].bitcast(FP8X4), rhs_scale=scales[:], start=True, stop=True,
                    )
                banks.append(bank)
            state[c] = banks

        def finish(c):
            lo, hi = CHUNKS[c]
            n = hi - lo
            per_bank = S // n
            rows = [bank[:, i : i + 2] for bank in state[c] for i in range(0, per_bank, 2)]
            for g, part in enumerate(rows):
                blocks = slice(2 * g, 2 * (g + 1))
                result = keep.tile([P, 2, n], F32, name=f"result{c}_{g}")
                nc.vector.tensor_tensor(result[:], part, res_sb[:, blocks, lo:hi], ALU.add)
                queue = nc.scalar if c == len(CHUNKS) - 1 and g == 0 else nc.sync
                queue.dma_start(out_view[:, blocks, lo:hi], result[:])

        closes = {units.index((3, lo, hi)): c for c, (lo, hi) in enumerate(CHUNKS)}
        for step in range(len(units) + 3):
            if step < len(units):
                fetch(*units[step])
            if 0 <= step - 1 < len(units):
                extremes(*units[step - 1])
            if step - 2 in closes:
                product(closes[step - 2])
            if step - 3 in closes:
                finish(closes[step - 3])
